import numpy as np
import ml_dtypes


def mxq(x, axis, fmt="e4m3"):
    dtype, down = {"e4m3": (ml_dtypes.float8_e4m3fn, 7), "e5m2": (ml_dtypes.float8_e5m2, 14)}[fmt]
    v = np.moveaxis(np.asarray(x, np.float32).astype(ml_dtypes.bfloat16).astype(np.float64), axis, -1)
    blocks = v.reshape(v.shape[:-1] + (-1, 32))
    amax = np.abs(blocks).max(-1, keepdims=True)
    byte = np.maximum(np.where(amax > 0, np.frexp(amax)[1] - 1 + 127, 0) - down, 1)
    scale = np.exp2(byte - 127.0)
    codes = (blocks / scale).astype(np.float32).astype(dtype).astype(np.float64)
    return np.moveaxis((codes * scale).reshape(v.shape), -1, axis)


WIDE = False


def mx_kscale(k, group=512):
    if not WIDE:
        return np.ones(k)
    levels = np.array([10, -10, 5, -5, 0])
    if group != 512:
        return np.exp2(np.random.permutation(np.resize(levels, k // group))).repeat(group)
    if k % 512:
        return np.exp2(np.random.permutation(np.resize(levels, k // 32))).repeat(32)
    a = np.empty((k // 512, 16))
    for p in range(k // 512):
        a[p, :8] = np.random.permutation(np.resize(levels, 8))
        for g in range(8):
            far = levels[np.abs(levels - a[p, g]) >= 10]
            a[p, g + 8] = far[np.random.randint(len(far))]
    return np.exp2(a.ravel()).repeat(32)


def f64(x):
    return np.asarray(x).astype(np.float64)


def sigmoid(v):
    return 1.0 / (1.0 + np.exp(-v))


G, D, M, O, N = 2, 256, 256, 256, 512


def sgn(shape):
    return np.random.uniform(0.5, 2.0, shape) * np.where(np.random.standard_normal(shape) < 0, -1.0, 1.0)


def setup_inputs():
    n = np.random.standard_normal
    s_d = mx_kscale(D, 0)
    s_m = mx_kscale(M, 0)
    return {
        "x": (n((G, D, N)) * s_d[:, None]).astype(np.float32),
        "w1": (n((G, D, M)) / np.sqrt(D) / s_d[:, None]).astype(np.float32),
        "w2": (n((G, D, M)) / np.sqrt(D) / s_d[:, None]).astype(np.float32),
        "tp": (np.random.uniform(0.5, 1.2, (G, M, 1))).astype(np.float32),
        "hs": (sgn((G, M, 1)) * s_m[:, None]).astype(np.float32),
        "wo2": (n((G, M, O)) / np.sqrt(M) / s_m[:, None]).astype(np.float32),
        "ob": (0.5 * n((G, O, 1))).astype(np.float32),
        "osc": (np.random.uniform(0.5, 2.0, (G, O, 1))).astype(np.float32),
    }


def reference(x, w1, w2, tp, hs, wo2, ob, osc):
    w1q = mxq(f64(w1), 1, "e4m3")
    xq = mxq(f64(x), 1, "e4m3")
    z1 = w1q.transpose(0, 2, 1) @ xq
    w2q = mxq(f64(w2), 1, "e4m3")
    z2 = w2q.transpose(0, 2, 1) @ xq
    s1 = z1 * f64(tp)
    ls = np.log(np.sum(np.exp(s1), axis=-1, keepdims=True))
    h = (s1 - ls + 6.0) * sigmoid(z2)
    hh = h * f64(hs)
    wo2q = mxq(f64(wo2), 1, "e4m3")
    hhq = mxq(hh, 1, "e4m3")
    y0 = wo2q.transpose(0, 2, 1) @ hhq
    y = np.tanh(y0 + f64(ob)) * f64(osc)
    return y

@@ -1,0 +1,224 @@
+import math
+from contextlib import ExitStack
+
+import concourse.mybir as mybir
+
+G, D, M, O, N = 2, 256, 256, 256, 512
+FLOPS = 2 * G * N * (2 * D * M + M * O)
+
+F32 = mybir.dt.float32
+BF16 = mybir.dt.bfloat16
+I32 = mybir.dt.int32
+U32 = mybir.dt.uint32
+U8 = mybir.dt.uint8
+FP8X4 = mybir.dt.float8_e4m3fn_x4
+ACT = mybir.ActivationFunctionType
+ALU = mybir.AluOpType
+
+P = 128
+PACK = 4
+ROWS = 64
+HALVES = 2
+QUAD = 32
+X_CHUNKS = 2
+GUESS_SLOPE = math.log(2.0) / 2.0**23
+GUESS_OFFSET = -88.0
+
+
+def interleave(copy, words, rows, first, last):
+    copy(
+        out=words[:, first:last, :].rearrange("p (c i) j -> p c j i", i=4),
+        in_=rows[:, :, first:last].rearrange("p j (c i) -> p c j i", i=4),
+    )
+
+
+def quantize(nc, codes, scales, words):
+    nc.vector.quantize_mx(out=codes.bitcast(FP8X4), scales=scales, in_=words.rearrange("p c j -> p (c j)"))
+
+
+def product(nc, bank, w_codes, w_scales, a_codes, a_scales, g, t):
+    rows = slice(ROWS * g, ROWS * (g + 1))
+    cols = slice(P * t, P * (t + 1))
+    nc.tensor.matmul_mx(
+        out=bank[:],
+        lhsT=w_codes[rows, cols].bitcast(FP8X4),
+        lhsT_scale=w_scales[rows, cols],
+        rhs=a_codes[rows, :].bitcast(FP8X4),
+        rhs_scale=a_scales[rows, :],
+        start=True,
+        stop=True,
+    )
+
+
+def tile_rows_frowlog_kernel(tc, x, w1, w2, tp, hs, wo2, ob, osc, out):
+    nc = tc.nc
+    tiles = [(g, t) for t in range(HALVES) for g in range(G)]
+    chunk = N // X_CHUNKS
+
+    with ExitStack() as ctx:
+        sb = ctx.enter_context(tc.tile_pool(name="sb", bufs=1))
+        ps = ctx.enter_context(tc.psum_pool(name="ps", bufs=1))
+        ctx.enter_context(tc.manual_schedule())
+
+        def sbuf(name, shape, dtype):
+            return sb.tile(shape, dtype, name=name, align_bytes=64)
+
+        def load_rows(name, src):
+            raw = sbuf(name, [P, PACK, src.shape[2]], F32)
+            nc.sync.dma_start(out=raw[:], in_=src.rearrange("g (p j) c -> (g p) j c", j=PACK))
+            return raw
+
+        vec_rows = sbuf("vec_rows", [P, P], F32)
+        nc.vector.memset(vec_rows[:], 0.0)
+        offset = sbuf("offset", [P, 1], F32)
+        nc.vector.memset(offset[:], GUESS_OFFSET)
+
+        w1_raw = load_rows("w1_raw", w1)
+        x_raw = [load_rows("x_raw%d" % h, x[:, :, chunk * h : chunk * (h + 1)]) for h in range(X_CHUNKS)]
+        w2_raw = load_rows("w2_raw", w2)
+        for v, vec in enumerate((tp, hs, ob, osc)):
+            nc.scalar.dma_start(
+                out=vec_rows[v:P:QUAD, :].rearrange("b (c i) -> b c i", i=QUAD),
+                in_=vec.rearrange("g (t b i) o -> b (g t) (i o)", t=HALVES, i=QUAD),
+            )
+        wo_raw = load_rows("wo_raw", wo2)
+
+        def mx_tiles(name, width):
+            return (
+                sbuf(name + "_words", [P, width, PACK], BF16),
+                sbuf(name + "_codes", [P, width], U32),
+                sbuf(name + "_scales", [P, width], U8),
+            )
+
+        w1_words, w1_codes, w1_scales = mx_tiles("w1", M)
+        w2_words, w2_codes, w2_scales = mx_tiles("w2", M)
+        wo_words, wo_codes, wo_scales = mx_tiles("wo", O)
+        hh_words, hh_codes, hh_scales = mx_tiles("hh", N)
+        x_words = [sbuf("x_words%d" % h, [P, chunk, PACK], BF16) for h in range(X_CHUNKS)]
+        x_codes = sbuf("x_codes", [P, N], U32)
+        x_scales = sbuf("x_scales", [P, N], U8)
+
+        def interleave_shared(words, rows, width, vector_cols):
+            interleave(nc.vector.tensor_copy, words, rows, 0, vector_cols)
+            interleave(nc.scalar.copy, words, rows, vector_cols, width)
+
+        interleave_shared(w1_words, w1_raw, M, 168)
+        quantize(nc, w1_codes[:], w1_scales[:], w1_words[:])
+
+        for h in range(X_CHUNKS):
+            cols = slice(chunk * h, chunk * (h + 1))
+            interleave_shared(x_words[h], x_raw[h], chunk, 168)
+            quantize(nc, x_codes[:, cols], x_scales[:, cols], x_words[h][:])
+
+        z1 = [ps.tile([P, N], F32, name="z1_%d" % k) for k in range(4)]
+        z2 = [ps.tile([P, N], F32, name="z2_%d" % k) for k in range(4)]
+        for k, (g, t) in enumerate(tiles):
+            product(nc, z1[k], w1_codes, w1_scales, x_codes, x_scales, g, t)
+
+        vec = sbuf("vec", [P, P], F32)
+        nc.vector.transpose(out=vec[:], in_=vec_rows[:])
+        interleave_shared(w2_words, w2_raw, M, 128)
+        neg_tp = sbuf("neg_tp", [P, 4], F32)
+        nc.vector.tensor_scalar(out=neg_tp[:], in0=vec[:, 0:P:QUAD], scalar1=-1.0, scalar2=None, op0=ALU.mult)
+        neg_half_hs = sbuf("neg_half_hs", [P, 4], F32)
+        nc.vector.tensor_scalar(out=neg_half_hs[:], in0=vec[:, 1:P:QUAD], scalar1=-0.5, scalar2=None, op0=ALU.mult)
+
+        neg_s = [sbuf("neg_s%d" % k, [P, N], F32) for k in range(4)]
+        gate = [sbuf("gate%d" % k, [P, N], F32) for k in range(4)]
+        half = [sbuf("half%d" % k, [P, N], F32) for k in range(4)]
+        neg_max = sbuf("neg_max", [P, 4], F32)
+        total = sbuf("total", [P, 4], F32)
+        for k, (g, t) in enumerate(tiles):
+            c = HALVES * g + t
+            nc.vector.tensor_scalar(
+                out=neg_s[k][:], in0=z1[k][:], scalar1=neg_tp[:, c : c + 1], scalar2=None,
+                op0=ALU.mult, op1=ALU.min, accum_out=neg_max[:, c : c + 1],
+            )
+            nc.scalar.activation(
+                out=half[k][:], in_=neg_s[k][:], func=ACT.Exp, scale=-1.0, bias=neg_max[:, c : c + 1],
+                accum_out=total[:, c : c + 1],
+            )
+            if k == 1:
+                quantize(nc, w2_codes[:], w2_scales[:], w2_words[:])
+                for k2, (g2, t2) in enumerate(tiles):
+                    product(nc, z2[k2], w2_codes, w2_scales, x_codes, x_scales, g2, t2)
+
+        def half_gate(k):
+            nc.scalar.activation(out=half[k][:], in_=z2[k][:], func=ACT.Tanh, scale=0.5)
+
+        def full_gate(k):
+            g, t = tiles[k]
+            c = HALVES * g + t
+            nc.vector.tensor_scalar(
+                out=gate[k][:], in0=half[k][:], scalar1=1.0, scalar2=neg_half_hs[:, c : c + 1],
+                op0=ALU.add, op1=ALU.mult,
+            )
+
+        def small(name):
+            return sbuf(name, [P, 4], F32)
+
+        bits = total[:].bitcast(U32)
+        near, guess = small("near"), small("guess")
+        nc.scalar.activation(out=near[:], in_=bits, func=ACT.Exp, scale=GUESS_SLOPE, bias=offset[:])
+        nc.scalar.activation(out=guess[:], in_=bits, func=ACT.Identity, scale=GUESS_SLOPE, bias=offset[:])
+        for k in range(4):
+            half_gate(k)
+
+        below, above, inverse, base = small("below"), small("above"), small("inverse"), small("base")
+        z, zz, shift = small("z"), small("zz"), small("shift")
+        nc.vector.tensor_tensor(out=below[:], in0=total[:], in1=near[:], op=ALU.add)
+        nc.vector.tensor_tensor(out=above[:], in0=total[:], in1=near[:], op=ALU.subtract)
+        nc.vector.reciprocal(out=inverse[:], in_=below[:])
+        nc.vector.scalar_tensor_tensor(
+            out=base[:], in0=guess[:], scalar=-6.0, in1=neg_max[:], op0=ALU.add, op1=ALU.subtract
+        )
+        nc.vector.tensor_tensor(out=z[:], in0=above[:], in1=inverse[:], op=ALU.mult)
+        full_gate(0)
+        nc.vector.tensor_tensor(out=zz[:], in0=z[:], in1=z[:], op=ALU.mult)
+        series = zz
+        for power, factor in ((5, zz), (3, zz), (1, z)):
+            step = small("series%d" % power)
+            nc.vector.scalar_tensor_tensor(
+                out=step[:], in0=series[:], scalar=7.0 / power, in1=factor[:], op0=ALU.add, op1=ALU.mult
+            )
+            series = step
+            if power == 5:
+                full_gate(1)
+            if power == 1:
+                full_gate(2)
+        nc.vector.scalar_tensor_tensor(
+            out=shift[:], in0=series[:], scalar=2.0 / 7.0, in1=base[:], op0=ALU.mult, op1=ALU.add
+        )
+        full_gate(3)
+
+        interleave(nc.scalar.copy, wo_words, wo_raw, 0, O)
+
+        hh_rows = sbuf("hh_rows", [P, PACK, N], BF16)
+        for k, (g, t) in enumerate(tiles):
+            c = HALVES * g + t
+            hh = sbuf("hh%d" % k, [P, N], BF16)
+            nc.vector.scalar_tensor_tensor(
+                out=hh[:], in0=neg_s[k][:], scalar=shift[:, c : c + 1], in1=gate[k][:], op0=ALU.add, op1=ALU.mult
+            )
+            first = ROWS * g + QUAD * t
+            nc.sync.dma_start(out=hh_rows[first : first + QUAD, :, :], in_=hh[:])
+
+        quantize(nc, wo_codes[:], wo_scales[:], wo_words[:])
+        interleave(nc.vector.tensor_copy, hh_words, hh_rows, 0, 256)
+        interleave(nc.scalar.copy, hh_words, hh_rows, 320, N)
+        interleave(nc.vector.tensor_copy, hh_words, hh_rows, 256, 320)
+        for h in range(2):
+            cols = slice(256 * h, 256 * (h + 1))
+            quantize(nc, hh_codes[:, cols], hh_scales[:, cols], hh_words[:, cols, :])
+
+        for k, (g, t) in enumerate(tiles):
+            product(nc, z1[k], wo_codes, wo_scales, hh_codes, hh_scales, g, t)
+        for k, (g, t) in enumerate(tiles):
+            c = QUAD * (HALVES * g + t)
+            squashed = sbuf("squashed%d" % k, [P, N], F32)
+            nc.scalar.activation(out=squashed[:], in_=z1[k][:], func=ACT.Tanh, bias=vec[:, c + 2 : c + 3])
+            result = sbuf("result%d" % k, [P, N], F32)
+            nc.vector.tensor_scalar(
+                out=result[:], in0=squashed[:], scalar1=vec[:, c + 3 : c + 4], scalar2=None, op0=ALU.mult
+            )
+            nc.sync.dma_start(out=out[g, P * t : P * (t + 1), :], in_=result[:])

@@ -8,7 +8,6 @@ FLOPS = 2 * G * N * (2 * D * M + M * O)
 
 F32 = mybir.dt.float32
 BF16 = mybir.dt.bfloat16
-I32 = mybir.dt.int32
 U32 = mybir.dt.uint32
 U8 = mybir.dt.uint8
 FP8X4 = mybir.dt.float8_e4m3fn_x4
@@ -18,11 +17,13 @@ ALU = mybir.AluOpType
 P = 128
 PACK = 4
 ROWS = 64
-HALVES = 2
 QUAD = 32
-X_CHUNKS = 2
+TILES = [(g, t) for t in range(2) for g in range(G)]
+HALF = N // 2
+CALL = 128
+VECTOR_COLS = 168
 GUESS_SLOPE = math.log(2.0) / 2.0**23
-GUESS_OFFSET = -88.0
+GUESS_OFFSET = 88.0
 
 
 def interleave(copy, words, rows, first, last):
@@ -36,24 +37,26 @@ def quantize(nc, codes, scales, words):
     nc.vector.quantize_mx(out=codes.bitcast(FP8X4), scales=scales, in_=words.rearrange("p c j -> p (c j)"))
 
 
-def product(nc, bank, w_codes, w_scales, a_codes, a_scales, g, t):
+def product(nc, sums, w_codes, w_scales, a_codes, a_scales, k, h):
+    g, t = TILES[k]
     rows = slice(ROWS * g, ROWS * (g + 1))
-    cols = slice(P * t, P * (t + 1))
-    nc.tensor.matmul_mx(
-        out=bank[:],
-        lhsT=w_codes[rows, cols].bitcast(FP8X4),
-        lhsT_scale=w_scales[rows, cols],
-        rhs=a_codes[rows, :].bitcast(FP8X4),
-        rhs_scale=a_scales[rows, :],
-        start=True,
-        stop=True,
-    )
+    w_cols = slice(P * t, P * (t + 1))
+    for first in range(0, HALF, CALL):
+        a_cols = slice(HALF * h + first, HALF * h + first + CALL)
+        nc.tensor.matmul_mx(
+            out=sums[:, first : first + CALL],
+            lhsT=w_codes[rows, w_cols].bitcast(FP8X4),
+            lhsT_scale=w_scales[rows, w_cols],
+            rhs=a_codes[rows, a_cols].bitcast(FP8X4),
+            rhs_scale=a_scales[rows, a_cols],
+            start=True,
+            stop=True,
+        )
 
 
 def tile_rows_frowlog_kernel(tc, x, w1, w2, tp, hs, wo2, ob, osc, out):
     nc = tc.nc
-    tiles = [(g, t) for t in range(HALVES) for g in range(G)]
-    chunk = N // X_CHUNKS
+    halves = [slice(HALF * h, HALF * (h + 1)) for h in range(2)]
 
     with ExitStack() as ctx:
         sb = ctx.enter_context(tc.tile_pool(name="sb", bufs=1))
@@ -63,10 +66,22 @@ def tile_rows_frowlog_kernel(tc, x, w1, w2, tp, hs, wo2, ob, osc, out):
         def sbuf(name, shape, dtype):
             return sb.tile(shape, dtype, name=name, align_bytes=64)
 
+        def small(name):
+            return sbuf(name, [P, len(TILES)], F32)
+
         def load_rows(name, src):
             raw = sbuf(name, [P, PACK, src.shape[2]], F32)
             nc.sync.dma_start(out=raw[:], in_=src.rearrange("g (p j) c -> (g p) j c", j=PACK))
             return raw
+
+        def mx_tiles(name, width):
+            return sbuf(name + "_codes", [P, width], U32), sbuf(name + "_scales", [P, width], U8)
+
+        def interleave_shared(name, rows, vector_cols):
+            words = sbuf(name, [P, HALF, PACK], BF16)
+            interleave(nc.vector.tensor_copy, words, rows, 0, vector_cols)
+            interleave(nc.scalar.copy, words, rows, vector_cols, HALF)
+            return words
 
         vec_rows = sbuf("vec_rows", [P, P], F32)
         nc.vector.memset(vec_rows[:], 0.0)
@@ -74,151 +89,138 @@ def tile_rows_frowlog_kernel(tc, x, w1, w2, tp, hs, wo2, ob, osc, out):
         nc.vector.memset(offset[:], GUESS_OFFSET)
 
         w1_raw = load_rows("w1_raw", w1)
-        x_raw = [load_rows("x_raw%d" % h, x[:, :, chunk * h : chunk * (h + 1)]) for h in range(X_CHUNKS)]
-        w2_raw = load_rows("w2_raw", w2)
-        for v, vec in enumerate((tp, hs, ob, osc)):
-            nc.scalar.dma_start(
+        for v, src in enumerate((tp, hs, ob, osc)):
+            nc.sync.dma_start(
                 out=vec_rows[v:P:QUAD, :].rearrange("b (c i) -> b c i", i=QUAD),
-                in_=vec.rearrange("g (t b i) o -> b (g t) (i o)", t=HALVES, i=QUAD),
+                in_=src.rearrange("g (t b i) o -> b (g t) (i o)", t=2, i=QUAD),
             )
+        x_raw = [load_rows("x_raw%d" % h, x[:, :, halves[h]]) for h in range(2)]
+        w2_raw = load_rows("w2_raw", w2)
         wo_raw = load_rows("wo_raw", wo2)
 
-        def mx_tiles(name, width):
-            return (
-                sbuf(name + "_words", [P, width, PACK], BF16),
-                sbuf(name + "_codes", [P, width], U32),
-                sbuf(name + "_scales", [P, width], U8),
-            )
+        w1_codes, w1_scales = mx_tiles("w1", M)
+        w2_codes, w2_scales = mx_tiles("w2", M)
+        wo_codes, wo_scales = mx_tiles("wo", O)
+        x_codes, x_scales = mx_tiles("x", N)
+        hh_codes, hh_scales = mx_tiles("hh", N)
 
-        w1_words, w1_codes, w1_scales = mx_tiles("w1", M)
-        w2_words, w2_codes, w2_scales = mx_tiles("w2", M)
-        wo_words, wo_codes, wo_scales = mx_tiles("wo", O)
-        hh_words, hh_codes, hh_scales = mx_tiles("hh", N)
-        x_words = [sbuf("x_words%d" % h, [P, chunk, PACK], BF16) for h in range(X_CHUNKS)]
-        x_codes = sbuf("x_codes", [P, N], U32)
-        x_scales = sbuf("x_scales", [P, N], U8)
-
-        def interleave_shared(words, rows, width, vector_cols):
-            interleave(nc.vector.tensor_copy, words, rows, 0, vector_cols)
-            interleave(nc.scalar.copy, words, rows, vector_cols, width)
-
-        interleave_shared(w1_words, w1_raw, M, 168)
+        w1_words = interleave_shared("w1_words", w1_raw, VECTOR_COLS)
+        vec = sbuf("vec", [P, P], F32)
+        nc.vector.transpose(out=vec[:], in_=vec_rows[:])
         quantize(nc, w1_codes[:], w1_scales[:], w1_words[:])
-
-        for h in range(X_CHUNKS):
-            cols = slice(chunk * h, chunk * (h + 1))
-            interleave_shared(x_words[h], x_raw[h], chunk, 168)
-            quantize(nc, x_codes[:, cols], x_scales[:, cols], x_words[h][:])
+        neg_tp, neg_half_hs = small("neg_tp"), small("neg_half_hs")
+        for scaled, v, factor in ((neg_tp, 0, -1.0), (neg_half_hs, 1, -0.5)):
+            nc.vector.tensor_scalar(
+                out=scaled[:].rearrange("p (t g) -> p g t", g=G),
+                in0=vec[:, v:P:QUAD].rearrange("p (g t) -> p g t", g=G),
+                scalar1=factor, scalar2=None, op0=ALU.mult,
+            )
 
         z1 = [ps.tile([P, N], F32, name="z1_%d" % k) for k in range(4)]
         z2 = [ps.tile([P, N], F32, name="z2_%d" % k) for k in range(4)]
-        for k, (g, t) in enumerate(tiles):
-            product(nc, z1[k], w1_codes, w1_scales, x_codes, x_scales, g, t)
+        for h in range(2):
+            x_words = interleave_shared("x_words%d" % h, x_raw[h], VECTOR_COLS)
+            quantize(nc, x_codes[:, halves[h]], x_scales[:, halves[h]], x_words[:])
+            for k in range(4):
+                product(nc, z1[k][:, halves[h]], w1_codes, w1_scales, x_codes, x_scales, k, h)
 
-        vec = sbuf("vec", [P, P], F32)
-        nc.vector.transpose(out=vec[:], in_=vec_rows[:])
-        interleave_shared(w2_words, w2_raw, M, 128)
-        neg_tp = sbuf("neg_tp", [P, 4], F32)
-        nc.vector.tensor_scalar(out=neg_tp[:], in0=vec[:, 0:P:QUAD], scalar1=-1.0, scalar2=None, op0=ALU.mult)
-        neg_half_hs = sbuf("neg_half_hs", [P, 4], F32)
-        nc.vector.tensor_scalar(out=neg_half_hs[:], in0=vec[:, 1:P:QUAD], scalar1=-0.5, scalar2=None, op0=ALU.mult)
+        w2_words = sbuf("w2_words", [P, M, PACK], BF16)
+        interleave(nc.scalar.copy, w2_words, w2_raw, M // 2, M)
 
         neg_s = [sbuf("neg_s%d" % k, [P, N], F32) for k in range(4)]
+        tanh_z2 = [sbuf("tanh_z2_%d" % k, [P, N], F32) for k in range(4)]
         gate = [sbuf("gate%d" % k, [P, N], F32) for k in range(4)]
-        half = [sbuf("half%d" % k, [P, N], F32) for k in range(4)]
-        neg_max = sbuf("neg_max", [P, 4], F32)
-        total = sbuf("total", [P, 4], F32)
-        for k, (g, t) in enumerate(tiles):
-            c = HALVES * g + t
+        neg_max, total = small("neg_max"), small("total")
+        for k in range(4):
             nc.vector.tensor_scalar(
-                out=neg_s[k][:], in0=z1[k][:], scalar1=neg_tp[:, c : c + 1], scalar2=None,
-                op0=ALU.mult, op1=ALU.min, accum_out=neg_max[:, c : c + 1],
+                out=neg_s[k][:], in0=z1[k][:], scalar1=neg_tp[:, k : k + 1], scalar2=None,
+                op0=ALU.mult, op1=ALU.min, accum_out=neg_max[:, k : k + 1],
             )
             nc.scalar.activation(
-                out=half[k][:], in_=neg_s[k][:], func=ACT.Exp, scale=-1.0, bias=neg_max[:, c : c + 1],
-                accum_out=total[:, c : c + 1],
+                out=tanh_z2[k][:], in_=neg_s[k][:], func=ACT.Exp, scale=-1.0, bias=neg_max[:, k : k + 1],
+                accum_out=total[:, k : k + 1],
             )
-            if k == 1:
-                quantize(nc, w2_codes[:], w2_scales[:], w2_words[:])
-                for k2, (g2, t2) in enumerate(tiles):
-                    product(nc, z2[k2], w2_codes, w2_scales, x_codes, x_scales, g2, t2)
 
-        def half_gate(k):
-            nc.scalar.activation(out=half[k][:], in_=z2[k][:], func=ACT.Tanh, scale=0.5)
+        interleave(nc.vector.tensor_copy, w2_words, w2_raw, 0, M // 2)
+        quantize(nc, w2_codes[:], w2_scales[:], w2_words[:])
+        for k in range(4):
+            for h in range(2):
+                product(nc, z2[k][:, halves[h]], w2_codes, w2_scales, x_codes, x_scales, k, h)
 
-        def full_gate(k):
-            g, t = tiles[k]
-            c = HALVES * g + t
+        bits = total[:].bitcast(U32)
+        undo, neg_guess = small("undo"), small("neg_guess")
+        nc.scalar.activation(out=undo[:], in_=bits, func=ACT.Exp, scale=-GUESS_SLOPE, bias=offset[:])
+        nc.scalar.activation(out=neg_guess[:], in_=bits, func=ACT.Identity, scale=-GUESS_SLOPE, bias=offset[:])
+        for k in range(4):
+            nc.scalar.activation(out=tanh_z2[k][:], in_=z2[k][:], func=ACT.Tanh, scale=0.5)
+
+        def make_gate(k):
             nc.vector.tensor_scalar(
-                out=gate[k][:], in0=half[k][:], scalar1=1.0, scalar2=neg_half_hs[:, c : c + 1],
+                out=gate[k][:], in0=tanh_z2[k][:], scalar1=1.0, scalar2=neg_half_hs[:, k : k + 1],
                 op0=ALU.add, op1=ALU.mult,
             )
 
-        def small(name):
-            return sbuf(name, [P, 4], F32)
+        def add_times(name, a, number, b):
+            result = small(name)
+            nc.vector.scalar_tensor_tensor(out=result[:], in0=a[:], scalar=number, in1=b[:], op0=ALU.add, op1=ALU.mult)
+            return result
 
-        bits = total[:].bitcast(U32)
-        near, guess = small("near"), small("guess")
-        nc.scalar.activation(out=near[:], in_=bits, func=ACT.Exp, scale=GUESS_SLOPE, bias=offset[:])
-        nc.scalar.activation(out=guess[:], in_=bits, func=ACT.Identity, scale=GUESS_SLOPE, bias=offset[:])
-        for k in range(4):
-            half_gate(k)
-
-        below, above, inverse, base = small("below"), small("above"), small("inverse"), small("base")
-        z, zz, shift = small("z"), small("zz"), small("shift")
-        nc.vector.tensor_tensor(out=below[:], in0=total[:], in1=near[:], op=ALU.add)
-        nc.vector.tensor_tensor(out=above[:], in0=total[:], in1=near[:], op=ALU.subtract)
+        w, base = small("w"), small("base")
+        w_plus, w_minus, inverse, shift = small("w_plus"), small("w_minus"), small("inverse"), small("shift")
+        nc.vector.tensor_tensor(out=w[:], in0=total[:], in1=undo[:], op=ALU.mult)
+        nc.vector.scalar_tensor_tensor(
+            out=base[:], in0=neg_guess[:], scalar=6.0, in1=neg_max[:], op0=ALU.add, op1=ALU.add
+        )
+        below_part = add_times("below_part", w, 8.0, w)
+        nc.vector.tensor_scalar(out=w_plus[:], in0=w[:], scalar1=1.0, scalar2=None, op0=ALU.add)
+        above_part = add_times("above_part", w, 38.0 / 11.0, w)
+        nc.vector.tensor_scalar(
+            out=w_minus[:], in0=w[:], scalar1=-1.0, scalar2=11.0 / 3.0, op0=ALU.add, op1=ALU.mult
+        )
+        below = add_times("below", below_part, 1.0, w_plus)
+        above = add_times("above", above_part, 1.0, w_minus)
+        make_gate(0)
         nc.vector.reciprocal(out=inverse[:], in_=below[:])
-        nc.vector.scalar_tensor_tensor(
-            out=base[:], in0=guess[:], scalar=-6.0, in1=neg_max[:], op0=ALU.add, op1=ALU.subtract
-        )
-        nc.vector.tensor_tensor(out=z[:], in0=above[:], in1=inverse[:], op=ALU.mult)
-        full_gate(0)
-        nc.vector.tensor_tensor(out=zz[:], in0=z[:], in1=z[:], op=ALU.mult)
-        series = zz
-        for power, factor in ((5, zz), (3, zz), (1, z)):
-            step = small("series%d" % power)
-            nc.vector.scalar_tensor_tensor(
-                out=step[:], in0=series[:], scalar=7.0 / power, in1=factor[:], op0=ALU.add, op1=ALU.mult
+        make_gate(1)
+        for k in range(4):
+            nc.vector.tensor_scalar(
+                out=shift[:, k : k + 1], in0=inverse[:, k : k + 1], scalar1=above[:, k : k + 1],
+                scalar2=base[:, k : k + 1], op0=ALU.mult, op1=ALU.subtract,
             )
-            series = step
-            if power == 5:
-                full_gate(1)
-            if power == 1:
-                full_gate(2)
-        nc.vector.scalar_tensor_tensor(
-            out=shift[:], in0=series[:], scalar=2.0 / 7.0, in1=base[:], op0=ALU.mult, op1=ALU.add
-        )
-        full_gate(3)
 
+        wo_words = sbuf("wo_words", [P, O, PACK], BF16)
         interleave(nc.scalar.copy, wo_words, wo_raw, 0, O)
 
-        hh_rows = sbuf("hh_rows", [P, PACK, N], BF16)
-        for k, (g, t) in enumerate(tiles):
-            c = HALVES * g + t
-            hh = sbuf("hh%d" % k, [P, N], BF16)
-            nc.vector.scalar_tensor_tensor(
-                out=hh[:], in0=neg_s[k][:], scalar=shift[:, c : c + 1], in1=gate[k][:], op0=ALU.add, op1=ALU.mult
-            )
-            first = ROWS * g + QUAD * t
-            nc.sync.dma_start(out=hh_rows[first : first + QUAD, :, :], in_=hh[:])
+        hh_rows = [sbuf("hh_rows%d" % h, [P, PACK, HALF], BF16) for h in range(2)]
+        for h in range(2):
+            for k, (g, t) in enumerate(TILES):
+                if h == 0 and k in (1, 2):
+                    make_gate(k + 1)
+                hh = sbuf("hh%d_%d" % (k, h), [P, HALF], BF16)
+                nc.vector.scalar_tensor_tensor(
+                    out=hh[:], in0=neg_s[k][:, halves[h]], scalar=shift[:, k : k + 1], in1=gate[k][:, halves[h]],
+                    op0=ALU.add, op1=ALU.mult,
+                )
+                first = ROWS * g + QUAD * t
+                nc.sync.dma_start(out=hh_rows[h][first : first + QUAD, :, :], in_=hh[:])
 
         quantize(nc, wo_codes[:], wo_scales[:], wo_words[:])
-        interleave(nc.vector.tensor_copy, hh_words, hh_rows, 0, 256)
-        interleave(nc.scalar.copy, hh_words, hh_rows, 320, N)
-        interleave(nc.vector.tensor_copy, hh_words, hh_rows, 256, 320)
+        y0 = [z1, z2]
         for h in range(2):
-            cols = slice(256 * h, 256 * (h + 1))
-            quantize(nc, hh_codes[:, cols], hh_scales[:, cols], hh_words[:, cols, :])
+            hh_words = interleave_shared("hh_words%d" % h, hh_rows[h], VECTOR_COLS)
+            quantize(nc, hh_codes[:, halves[h]], hh_scales[:, halves[h]], hh_words[:])
+            for k in range(4):
+                product(nc, y0[h][k][:, 0:HALF], wo_codes, wo_scales, hh_codes, hh_scales, k, h)
 
-        for k, (g, t) in enumerate(tiles):
-            product(nc, z1[k], wo_codes, wo_scales, hh_codes, hh_scales, g, t)
-        for k, (g, t) in enumerate(tiles):
-            c = QUAD * (HALVES * g + t)
-            squashed = sbuf("squashed%d" % k, [P, N], F32)
-            nc.scalar.activation(out=squashed[:], in_=z1[k][:], func=ACT.Tanh, bias=vec[:, c + 2 : c + 3])
-            result = sbuf("result%d" % k, [P, N], F32)
-            nc.vector.tensor_scalar(
-                out=result[:], in0=squashed[:], scalar1=vec[:, c + 3 : c + 4], scalar2=None, op0=ALU.mult
-            )
-            nc.sync.dma_start(out=out[g, P * t : P * (t + 1), :], in_=result[:])
+        for h in range(2):
+            for k, (g, t) in enumerate(TILES):
+                c = QUAD * (2 * g + t)
+                squashed = sbuf("squashed%d_%d" % (k, h), [P, HALF], F32)
+                nc.scalar.activation(
+                    out=squashed[:], in_=y0[h][k][:, 0:HALF], func=ACT.Tanh, bias=vec[:, c + 2 : c + 3]
+                )
+                result = sbuf("result%d_%d" % (k, h), [P, HALF], F32)
+                nc.vector.tensor_scalar(
+                    out=result[:], in0=squashed[:], scalar1=vec[:, c + 3 : c + 4], scalar2=None, op0=ALU.mult
+                )
+                nc.sync.dma_start(out=out[g, P * t : P * (t + 1), halves[h]], in_=result[:])

@@ -22,6 +22,9 @@ TILES = [(g, t) for t in range(2) for g in range(G)]
 HALF = N // 2
 CALL = 128
 VECTOR_COLS = 168
+X_VECTOR_COLS = 312
+W1_VECTOR_COLS = 80
+W2_VECTOR_COLS = 48
 GUESS_SLOPE = math.log(2.0) / 2.0**23
 GUESS_OFFSET = 88.0
 
@@ -77,24 +80,18 @@ def tile_rows_frowlog_kernel(tc, x, w1, w2, tp, hs, wo2, ob, osc, out):
         def mx_tiles(name, width):
             return sbuf(name + "_codes", [P, width], U32), sbuf(name + "_scales", [P, width], U8)
 
-        def interleave_shared(name, rows, vector_cols):
-            words = sbuf(name, [P, HALF, PACK], BF16)
-            interleave(nc.vector.tensor_copy, words, rows, 0, vector_cols)
-            interleave(nc.scalar.copy, words, rows, vector_cols, HALF)
-            return words
-
         vec_rows = sbuf("vec_rows", [P, P], F32)
         nc.vector.memset(vec_rows[:], 0.0)
         offset = sbuf("offset", [P, 1], F32)
         nc.vector.memset(offset[:], GUESS_OFFSET)
 
-        w1_raw = load_rows("w1_raw", w1)
+        x_raw = load_rows("x_raw", x)
         for v, src in enumerate((tp, hs, ob, osc)):
             nc.sync.dma_start(
                 out=vec_rows[v:P:QUAD, :].rearrange("b (c i) -> b c i", i=QUAD),
                 in_=src.rearrange("g (t b i) o -> b (g t) (i o)", t=2, i=QUAD),
             )
-        x_raw = [load_rows("x_raw%d" % h, x[:, :, halves[h]]) for h in range(2)]
+        w1_raw = load_rows("w1_raw", w1)
         w2_raw = load_rows("w2_raw", w2)
         wo_raw = load_rows("wo_raw", wo2)
 
@@ -104,10 +101,20 @@ def tile_rows_frowlog_kernel(tc, x, w1, w2, tp, hs, wo2, ob, osc, out):
         x_codes, x_scales = mx_tiles("x", N)
         hh_codes, hh_scales = mx_tiles("hh", N)
 
-        w1_words = interleave_shared("w1_words", w1_raw, VECTOR_COLS)
+        x_words = sbuf("x_words", [P, N, PACK], BF16)
+        interleave(nc.vector.tensor_copy, x_words, x_raw, 0, HALF)
+        interleave(nc.scalar.copy, x_words, x_raw, X_VECTOR_COLS, N)
+        interleave(nc.vector.tensor_copy, x_words, x_raw, HALF, X_VECTOR_COLS)
+        quantize(nc, x_codes[:, halves[0]], x_scales[:, halves[0]], x_words[:, halves[0], :])
+        w1_words = sbuf("w1_words", [P, M, PACK], BF16)
+        interleave(nc.vector.tensor_copy, w1_words, w1_raw, 0, W1_VECTOR_COLS)
+        interleave(nc.scalar.copy, w1_words, w1_raw, W1_VECTOR_COLS, P)
+        interleave(nc.scalar.copy, w1_words, w1_raw, P, M)
+        quantize(nc, x_codes[:, halves[1]], x_scales[:, halves[1]], x_words[:, halves[1], :])
+        quantize(nc, w1_codes[:, 0:P], w1_scales[:, 0:P], w1_words[:, 0:P, :])
         vec = sbuf("vec", [P, P], F32)
         nc.vector.transpose(out=vec[:], in_=vec_rows[:])
-        quantize(nc, w1_codes[:], w1_scales[:], w1_words[:])
+        quantize(nc, w1_codes[:, P:M], w1_scales[:, P:M], w1_words[:, P:M, :])
         neg_tp, neg_half_hs = small("neg_tp"), small("neg_half_hs")
         for scaled, v, factor in ((neg_tp, 0, -1.0), (neg_half_hs, 1, -0.5)):
             nc.vector.tensor_scalar(
@@ -116,16 +123,15 @@ def tile_rows_frowlog_kernel(tc, x, w1, w2, tp, hs, wo2, ob, osc, out):
                 scalar1=factor, scalar2=None, op0=ALU.mult,
             )
 
-        z1 = [ps.tile([P, N], F32, name="z1_%d" % k) for k in range(4)]
-        z2 = [ps.tile([P, N], F32, name="z2_%d" % k) for k in range(4)]
-        for h in range(2):
-            x_words = interleave_shared("x_words%d" % h, x_raw[h], VECTOR_COLS)
-            quantize(nc, x_codes[:, halves[h]], x_scales[:, halves[h]], x_words[:])
-            for k in range(4):
+        banks = [[ps.tile([P, N], F32, name="bank%d_%d" % (h, k)) for k in range(4)] for h in range(2)]
+        z1 = banks[1]
+        for k in range(4):
+            for h in range(2):
                 product(nc, z1[k][:, halves[h]], w1_codes, w1_scales, x_codes, x_scales, k, h)
 
         w2_words = sbuf("w2_words", [P, M, PACK], BF16)
-        interleave(nc.scalar.copy, w2_words, w2_raw, M // 2, M)
+        interleave(nc.vector.tensor_copy, w2_words, w2_raw, 0, W2_VECTOR_COLS)
+        interleave(nc.scalar.copy, w2_words, w2_raw, W2_VECTOR_COLS, M)
 
         neg_s = [sbuf("neg_s%d" % k, [P, N], F32) for k in range(4)]
         tanh_z2 = [sbuf("tanh_z2_%d" % k, [P, N], F32) for k in range(4)]
@@ -141,23 +147,25 @@ def tile_rows_frowlog_kernel(tc, x, w1, w2, tp, hs, wo2, ob, osc, out):
                 accum_out=total[:, k : k + 1],
             )
 
-        interleave(nc.vector.tensor_copy, w2_words, w2_raw, 0, M // 2)
         quantize(nc, w2_codes[:], w2_scales[:], w2_words[:])
-        for k in range(4):
-            for h in range(2):
-                product(nc, z2[k][:, halves[h]], w2_codes, w2_scales, x_codes, x_scales, k, h)
+        for h in range(2):
+            for k in range(4):
+                product(nc, banks[h][k][:, 0:HALF], w2_codes, w2_scales, x_codes, x_scales, k, h)
 
         bits = total[:].bitcast(U32)
         undo, neg_guess = small("undo"), small("neg_guess")
         nc.scalar.activation(out=undo[:], in_=bits, func=ACT.Exp, scale=-GUESS_SLOPE, bias=offset[:])
         nc.scalar.activation(out=neg_guess[:], in_=bits, func=ACT.Identity, scale=-GUESS_SLOPE, bias=offset[:])
-        for k in range(4):
-            nc.scalar.activation(out=tanh_z2[k][:], in_=z2[k][:], func=ACT.Tanh, scale=0.5)
+        for h in range(2):
+            for k in range(4):
+                nc.scalar.activation(
+                    out=tanh_z2[k][:, halves[h]], in_=banks[h][k][:, 0:HALF], func=ACT.Tanh, scale=0.5
+                )
 
-        def make_gate(k):
+        def make_gate(k, h):
             nc.vector.tensor_scalar(
-                out=gate[k][:], in0=tanh_z2[k][:], scalar1=1.0, scalar2=neg_half_hs[:, k : k + 1],
-                op0=ALU.add, op1=ALU.mult,
+                out=gate[k][:, halves[h]], in0=tanh_z2[k][:, halves[h]], scalar1=1.0,
+                scalar2=neg_half_hs[:, k : k + 1], op0=ALU.add, op1=ALU.mult,
             )
 
         def add_times(name, a, number, b):
@@ -177,15 +185,23 @@ def tile_rows_frowlog_kernel(tc, x, w1, w2, tp, hs, wo2, ob, osc, out):
         nc.vector.tensor_scalar(
             out=w_minus[:], in0=w[:], scalar1=-1.0, scalar2=11.0 / 3.0, op0=ALU.add, op1=ALU.mult
         )
+        make_gate(0, 0)
         below = add_times("below", below_part, 1.0, w_plus)
         above = add_times("above", above_part, 1.0, w_minus)
-        make_gate(0)
+        make_gate(1, 0)
         nc.vector.reciprocal(out=inverse[:], in_=below[:])
-        make_gate(1)
+        make_gate(2, 0)
         for k in range(4):
             nc.vector.tensor_scalar(
                 out=shift[:, k : k + 1], in0=inverse[:, k : k + 1], scalar1=above[:, k : k + 1],
                 scalar2=base[:, k : k + 1], op0=ALU.mult, op1=ALU.subtract,
+            )
+        make_gate(3, 0)
+
+        for k in range(4):
+            nc.scalar.activation(
+                out=gate[k][:, halves[1]], in_=tanh_z2[k][:, halves[1]], func=ACT.Identity,
+                scale=neg_half_hs[:, k : k + 1], bias=neg_half_hs[:, k : k + 1],
             )
 
         wo_words = sbuf("wo_words", [P, O, PACK], BF16)
@@ -194,8 +210,6 @@ def tile_rows_frowlog_kernel(tc, x, w1, w2, tp, hs, wo2, ob, osc, out):
         hh_rows = [sbuf("hh_rows%d" % h, [P, PACK, HALF], BF16) for h in range(2)]
         for h in range(2):
             for k, (g, t) in enumerate(TILES):
-                if h == 0 and k in (1, 2):
-                    make_gate(k + 1)
                 hh = sbuf("hh%d_%d" % (k, h), [P, HALF], BF16)
                 nc.vector.scalar_tensor_tensor(
                     out=hh[:], in0=neg_s[k][:, halves[h]], scalar=shift[:, k : k + 1], in1=gate[k][:, halves[h]],
@@ -204,20 +218,27 @@ def tile_rows_frowlog_kernel(tc, x, w1, w2, tp, hs, wo2, ob, osc, out):
                 first = ROWS * g + QUAD * t
                 nc.sync.dma_start(out=hh_rows[h][first : first + QUAD, :, :], in_=hh[:])
 
-        quantize(nc, wo_codes[:], wo_scales[:], wo_words[:])
-        y0 = [z1, z2]
         for h in range(2):
-            hh_words = interleave_shared("hh_words%d" % h, hh_rows[h], VECTOR_COLS)
-            quantize(nc, hh_codes[:, halves[h]], hh_scales[:, halves[h]], hh_words[:])
+            hh_words = sbuf("hh_words%d" % h, [P, HALF, PACK], BF16)
+            interleave(nc.vector.tensor_copy, hh_words, hh_rows[h], 0, CALL)
+            if h == 0:
+                interleave(nc.scalar.copy, hh_words, hh_rows[h], VECTOR_COLS, HALF)
+                interleave(nc.vector.tensor_copy, hh_words, hh_rows[h], CALL, VECTOR_COLS)
+                quantize(nc, wo_codes[:], wo_scales[:], wo_words[:])
+            else:
+                interleave(nc.vector.tensor_copy, hh_words, hh_rows[h], CALL, HALF)
+            for first in range(0, HALF, CALL):
+                cols = slice(HALF * h + first, HALF * h + first + CALL)
+                quantize(nc, hh_codes[:, cols], hh_scales[:, cols], hh_words[:, first : first + CALL, :])
             for k in range(4):
-                product(nc, y0[h][k][:, 0:HALF], wo_codes, wo_scales, hh_codes, hh_scales, k, h)
+                product(nc, banks[h][k][:, 0:HALF], wo_codes, wo_scales, hh_codes, hh_scales, k, h)
 
         for h in range(2):
             for k, (g, t) in enumerate(TILES):
                 c = QUAD * (2 * g + t)
                 squashed = sbuf("squashed%d_%d" % (k, h), [P, HALF], F32)
                 nc.scalar.activation(
-                    out=squashed[:], in_=y0[h][k][:, 0:HALF], func=ACT.Tanh, bias=vec[:, c + 2 : c + 3]
+                    out=squashed[:], in_=banks[h][k][:, 0:HALF], func=ACT.Tanh, bias=vec[:, c + 2 : c + 3]
                 )
                 result = sbuf("result%d_%d" % (k, h), [P, HALF], F32)
                 nc.vector.tensor_scalar(

@@ -86,12 +86,12 @@ def tile_rows_frowlog_kernel(tc, x, w1, w2, tp, hs, wo2, ob, osc, out):
         nc.vector.memset(offset[:], GUESS_OFFSET)
 
         x_raw = load_rows("x_raw", x)
+        w1_raw = load_rows("w1_raw", w1)
         for v, src in enumerate((tp, hs, ob, osc)):
             nc.sync.dma_start(
                 out=vec_rows[v:P:QUAD, :].rearrange("b (c i) -> b c i", i=QUAD),
                 in_=src.rearrange("g (t b i) o -> b (g t) (i o)", t=2, i=QUAD),
             )
-        w1_raw = load_rows("w1_raw", w1)
         w2_raw = load_rows("w2_raw", w2)
         wo_raw = load_rows("wo_raw", wo2)
 
@@ -137,6 +137,16 @@ def tile_rows_frowlog_kernel(tc, x, w1, w2, tp, hs, wo2, ob, osc, out):
         tanh_z2 = [sbuf("tanh_z2_%d" % k, [P, N], F32) for k in range(4)]
         gate = [sbuf("gate%d" % k, [P, N], F32) for k in range(4)]
         neg_max, total = small("neg_max"), small("total")
+        undo, neg_guess = small("undo"), small("neg_guess")
+        pairs = [slice(0, 2), slice(2, 4)]
+
+        def guess_log(pair):
+            bits = total[:, pair].bitcast(U32)
+            nc.scalar.activation(out=undo[:, pair], in_=bits, func=ACT.Exp, scale=-GUESS_SLOPE, bias=offset[:])
+            nc.scalar.activation(
+                out=neg_guess[:, pair], in_=bits, func=ACT.Identity, scale=-GUESS_SLOPE, bias=offset[:]
+            )
+
         for k in range(4):
             nc.vector.tensor_scalar(
                 out=neg_s[k][:], in0=z1[k][:], scalar1=neg_tp[:, k : k + 1], scalar2=None,
@@ -146,16 +156,13 @@ def tile_rows_frowlog_kernel(tc, x, w1, w2, tp, hs, wo2, ob, osc, out):
                 out=tanh_z2[k][:], in_=neg_s[k][:], func=ACT.Exp, scale=-1.0, bias=neg_max[:, k : k + 1],
                 accum_out=total[:, k : k + 1],
             )
+            if k >= 2:
+                guess_log(pairs[k - 2])
 
         quantize(nc, w2_codes[:], w2_scales[:], w2_words[:])
         for h in range(2):
             for k in range(4):
                 product(nc, banks[h][k][:, 0:HALF], w2_codes, w2_scales, x_codes, x_scales, k, h)
-
-        bits = total[:].bitcast(U32)
-        undo, neg_guess = small("undo"), small("neg_guess")
-        nc.scalar.activation(out=undo[:], in_=bits, func=ACT.Exp, scale=-GUESS_SLOPE, bias=offset[:])
-        nc.scalar.activation(out=neg_guess[:], in_=bits, func=ACT.Identity, scale=-GUESS_SLOPE, bias=offset[:])
         for h in range(2):
             for k in range(4):
                 nc.scalar.activation(
@@ -168,55 +175,79 @@ def tile_rows_frowlog_kernel(tc, x, w1, w2, tp, hs, wo2, ob, osc, out):
                 scalar2=neg_half_hs[:, k : k + 1], op0=ALU.add, op1=ALU.mult,
             )
 
-        def add_times(name, a, number, b):
-            result = small(name)
-            nc.vector.scalar_tensor_tensor(out=result[:], in0=a[:], scalar=number, in1=b[:], op0=ALU.add, op1=ALU.mult)
-            return result
+        def add_times(result, a, number, b):
+            nc.vector.scalar_tensor_tensor(out=result, in0=a, scalar=number, in1=b, op0=ALU.add, op1=ALU.mult)
 
-        w, base = small("w"), small("base")
-        w_plus, w_minus, inverse, shift = small("w_plus"), small("w_minus"), small("inverse"), small("shift")
-        nc.vector.tensor_tensor(out=w[:], in0=total[:], in1=undo[:], op=ALU.mult)
-        nc.vector.scalar_tensor_tensor(
-            out=base[:], in0=neg_guess[:], scalar=6.0, in1=neg_max[:], op0=ALU.add, op1=ALU.add
-        )
-        below_part = add_times("below_part", w, 8.0, w)
-        nc.vector.tensor_scalar(out=w_plus[:], in0=w[:], scalar1=1.0, scalar2=None, op0=ALU.add)
-        above_part = add_times("above_part", w, 38.0 / 11.0, w)
-        nc.vector.tensor_scalar(
-            out=w_minus[:], in0=w[:], scalar1=-1.0, scalar2=11.0 / 3.0, op0=ALU.add, op1=ALU.mult
-        )
-        make_gate(0, 0)
-        below = add_times("below", below_part, 1.0, w_plus)
-        above = add_times("above", above_part, 1.0, w_minus)
-        make_gate(1, 0)
-        nc.vector.reciprocal(out=inverse[:], in_=below[:])
-        make_gate(2, 0)
-        for k in range(4):
-            nc.vector.tensor_scalar(
-                out=shift[:, k : k + 1], in0=inverse[:, k : k + 1], scalar1=above[:, k : k + 1],
-                scalar2=base[:, k : k + 1], op0=ALU.mult, op1=ALU.subtract,
+        w, base, w_plus, w_minus = small("w"), small("base"), small("w_plus"), small("w_minus")
+        below_part, above_part, below, above = small("below_part"), small("above_part"), small("below"), small("above")
+        inverse, shift = small("inverse"), small("shift")
+
+        def log_step(step, c):
+            if step == 0:
+                nc.vector.tensor_tensor(out=w[:, c], in0=total[:, c], in1=undo[:, c], op=ALU.mult)
+                nc.vector.scalar_tensor_tensor(
+                    out=base[:, c], in0=neg_guess[:, c], scalar=6.0, in1=neg_max[:, c], op0=ALU.add, op1=ALU.add
+                )
+            elif step == 1:
+                add_times(below_part[:, c], w[:, c], 8.0, w[:, c])
+                nc.vector.tensor_scalar(out=w_plus[:, c], in0=w[:, c], scalar1=1.0, scalar2=None, op0=ALU.add)
+                add_times(above_part[:, c], w[:, c], 38.0 / 11.0, w[:, c])
+                nc.vector.tensor_scalar(
+                    out=w_minus[:, c], in0=w[:, c], scalar1=-1.0, scalar2=11.0 / 3.0, op0=ALU.add, op1=ALU.mult
+                )
+            elif step == 2:
+                add_times(below[:, c], below_part[:, c], 1.0, w_plus[:, c])
+                add_times(above[:, c], above_part[:, c], 1.0, w_minus[:, c])
+            elif step == 3:
+                nc.vector.reciprocal(out=inverse[:, c], in_=below[:, c])
+            else:
+                for k in range(c.start, c.stop):
+                    nc.vector.tensor_scalar(
+                        out=shift[:, k : k + 1], in0=inverse[:, k : k + 1], scalar1=above[:, k : k + 1],
+                        scalar2=base[:, k : k + 1], op0=ALU.mult, op1=ALU.subtract,
+                    )
+
+        hh_rows = [sbuf("hh_rows%d" % h, [P, PACK, HALF], BF16) for h in range(2)]
+
+        def make_hh(k, h):
+            g, t = TILES[k]
+            hh = sbuf("hh%d_%d" % (k, h), [P, HALF], BF16)
+            nc.vector.scalar_tensor_tensor(
+                out=hh[:], in0=neg_s[k][:, halves[h]], scalar=shift[:, k : k + 1], in1=gate[k][:, halves[h]],
+                op0=ALU.add, op1=ALU.mult,
             )
-        make_gate(3, 0)
+            first = ROWS * g + QUAD * t
+            nc.sync.dma_start(out=hh_rows[h][first : first + QUAD, :, :], in_=hh[:])
 
-        for k in range(4):
+        early, late = pairs
+        for step in range(3):
+            log_step(step, early)
+        log_step(0, late)
+        log_step(3, early)
+        log_step(1, late)
+        make_gate(0, 0)
+        log_step(4, early)
+        log_step(2, late)
+        make_gate(1, 0)
+        log_step(3, late)
+        make_hh(0, 0)
+        log_step(4, late)
+        make_gate(2, 0)
+        make_hh(1, 0)
+        make_gate(3, 0)
+        make_hh(2, 0)
+        make_gate(0, 1)
+        make_hh(3, 0)
+        for k in (1, 2, 3):
             nc.scalar.activation(
                 out=gate[k][:, halves[1]], in_=tanh_z2[k][:, halves[1]], func=ACT.Identity,
                 scale=neg_half_hs[:, k : k + 1], bias=neg_half_hs[:, k : k + 1],
             )
+        for k in range(4):
+            make_hh(k, 1)
 
         wo_words = sbuf("wo_words", [P, O, PACK], BF16)
         interleave(nc.scalar.copy, wo_words, wo_raw, 0, O)
-
-        hh_rows = [sbuf("hh_rows%d" % h, [P, PACK, HALF], BF16) for h in range(2)]
-        for h in range(2):
-            for k, (g, t) in enumerate(TILES):
-                hh = sbuf("hh%d_%d" % (k, h), [P, HALF], BF16)
-                nc.vector.scalar_tensor_tensor(
-                    out=hh[:], in0=neg_s[k][:, halves[h]], scalar=shift[:, k : k + 1], in1=gate[k][:, halves[h]],
-                    op0=ALU.add, op1=ALU.mult,
-                )
-                first = ROWS * g + QUAD * t
-                nc.sync.dma_start(out=hh_rows[h][first : first + QUAD, :, :], in_=hh[:])
 
         for h in range(2):
             hh_words = sbuf("hh_words%d" % h, [P, HALF, PACK], BF16)

import math
from contextlib import ExitStack

import concourse.mybir as mybir

G, D, M, O, N = 2, 256, 256, 256, 512
FLOPS = 2 * G * N * (2 * D * M + M * O)

F32 = mybir.dt.float32
BF16 = mybir.dt.bfloat16
U32 = mybir.dt.uint32
U8 = mybir.dt.uint8
FP8X4 = mybir.dt.float8_e4m3fn_x4
ACT = mybir.ActivationFunctionType
ALU = mybir.AluOpType

P = 128
PACK = 4
ROWS = 64
QUAD = 32
TILES = [(g, t) for t in range(2) for g in range(G)]
HALF = N // 2
CALL = 128
VECTOR_COLS = 168
X_VECTOR_COLS = 312
W1_VECTOR_COLS = 80
W2_VECTOR_COLS = 48
GUESS_SLOPE = math.log(2.0) / 2.0**23
GUESS_OFFSET = 88.0


def interleave(copy, words, rows, first, last):
    copy(
        out=words[:, first:last, :].rearrange("p (c i) j -> p c j i", i=4),
        in_=rows[:, :, first:last].rearrange("p j (c i) -> p c j i", i=4),
    )


def quantize(nc, codes, scales, words):
    nc.vector.quantize_mx(out=codes.bitcast(FP8X4), scales=scales, in_=words.rearrange("p c j -> p (c j)"))


def product(nc, sums, w_codes, w_scales, a_codes, a_scales, k, h):
    g, t = TILES[k]
    rows = slice(ROWS * g, ROWS * (g + 1))
    w_cols = slice(P * t, P * (t + 1))
    for first in range(0, HALF, CALL):
        a_cols = slice(HALF * h + first, HALF * h + first + CALL)
        nc.tensor.matmul_mx(
            out=sums[:, first : first + CALL],
            lhsT=w_codes[rows, w_cols].bitcast(FP8X4),
            lhsT_scale=w_scales[rows, w_cols],
            rhs=a_codes[rows, a_cols].bitcast(FP8X4),
            rhs_scale=a_scales[rows, a_cols],
            start=True,
            stop=True,
        )


def tile_rows_frowlog_kernel(tc, x, w1, w2, tp, hs, wo2, ob, osc, out):
    nc = tc.nc
    halves = [slice(HALF * h, HALF * (h + 1)) for h in range(2)]

    with ExitStack() as ctx:
        sb = ctx.enter_context(tc.tile_pool(name="sb", bufs=1))
        ps = ctx.enter_context(tc.psum_pool(name="ps", bufs=1))
        ctx.enter_context(tc.manual_schedule())

        def sbuf(name, shape, dtype):
            return sb.tile(shape, dtype, name=name, align_bytes=64)

        def small(name):
            return sbuf(name, [P, len(TILES)], F32)

        def load_rows(name, src):
            raw = sbuf(name, [P, PACK, src.shape[2]], F32)
            nc.sync.dma_start(out=raw[:], in_=src.rearrange("g (p j) c -> (g p) j c", j=PACK))
            return raw

        def mx_tiles(name, width):
            return sbuf(name + "_codes", [P, width], U32), sbuf(name + "_scales", [P, width], U8)

        vec_rows = sbuf("vec_rows", [P, P], F32)
        nc.vector.memset(vec_rows[:], 0.0)
        offset = sbuf("offset", [P, 1], F32)
        nc.vector.memset(offset[:], GUESS_OFFSET)

        x_raw = load_rows("x_raw", x)
        w1_raw = load_rows("w1_raw", w1)
        for v, src in enumerate((tp, hs, ob, osc)):
            nc.sync.dma_start(
                out=vec_rows[v:P:QUAD, :].rearrange("b (c i) -> b c i", i=QUAD),
                in_=src.rearrange("g (t b i) o -> b (g t) (i o)", t=2, i=QUAD),
            )
        w2_raw = load_rows("w2_raw", w2)
        wo_raw = load_rows("wo_raw", wo2)

        w1_codes, w1_scales = mx_tiles("w1", M)
        w2_codes, w2_scales = mx_tiles("w2", M)
        wo_codes, wo_scales = mx_tiles("wo", O)
        x_codes, x_scales = mx_tiles("x", N)
        hh_codes, hh_scales = mx_tiles("hh", N)

        x_words = sbuf("x_words", [P, N, PACK], BF16)
        interleave(nc.vector.tensor_copy, x_words, x_raw, 0, HALF)
        interleave(nc.scalar.copy, x_words, x_raw, X_VECTOR_COLS, N)
        interleave(nc.vector.tensor_copy, x_words, x_raw, HALF, X_VECTOR_COLS)
        quantize(nc, x_codes[:, halves[0]], x_scales[:, halves[0]], x_words[:, halves[0], :])
        w1_words = sbuf("w1_words", [P, M, PACK], BF16)
        interleave(nc.vector.tensor_copy, w1_words, w1_raw, 0, W1_VECTOR_COLS)
        interleave(nc.scalar.copy, w1_words, w1_raw, W1_VECTOR_COLS, P)
        interleave(nc.scalar.copy, w1_words, w1_raw, P, M)
        quantize(nc, x_codes[:, halves[1]], x_scales[:, halves[1]], x_words[:, halves[1], :])
        quantize(nc, w1_codes[:, 0:P], w1_scales[:, 0:P], w1_words[:, 0:P, :])
        vec = sbuf("vec", [P, P], F32)
        nc.vector.transpose(out=vec[:], in_=vec_rows[:])
        quantize(nc, w1_codes[:, P:M], w1_scales[:, P:M], w1_words[:, P:M, :])
        neg_tp, neg_half_hs = small("neg_tp"), small("neg_half_hs")
        for scaled, v, factor in ((neg_tp, 0, -1.0), (neg_half_hs, 1, -0.5)):
            nc.vector.tensor_scalar(
                out=scaled[:].rearrange("p (t g) -> p g t", g=G),
                in0=vec[:, v:P:QUAD].rearrange("p (g t) -> p g t", g=G),
                scalar1=factor, scalar2=None, op0=ALU.mult,
            )

        banks = [[ps.tile([P, N], F32, name="bank%d_%d" % (h, k)) for k in range(4)] for h in range(2)]
        z1 = banks[1]
        for k in range(4):
            for h in range(2):
                product(nc, z1[k][:, halves[h]], w1_codes, w1_scales, x_codes, x_scales, k, h)

        w2_words = sbuf("w2_words", [P, M, PACK], BF16)
        interleave(nc.vector.tensor_copy, w2_words, w2_raw, 0, W2_VECTOR_COLS)
        interleave(nc.scalar.copy, w2_words, w2_raw, W2_VECTOR_COLS, M)

        neg_s = [sbuf("neg_s%d" % k, [P, N], F32) for k in range(4)]
        tanh_z2 = [sbuf("tanh_z2_%d" % k, [P, N], F32) for k in range(4)]
        gate = [sbuf("gate%d" % k, [P, N], F32) for k in range(4)]
        neg_max, total = small("neg_max"), small("total")
        undo, neg_guess = small("undo"), small("neg_guess")
        pairs = [slice(0, 2), slice(2, 4)]

        def guess_log(pair):
            bits = total[:, pair].bitcast(U32)
            nc.scalar.activation(out=undo[:, pair], in_=bits, func=ACT.Exp, scale=-GUESS_SLOPE, bias=offset[:])
            nc.scalar.activation(
                out=neg_guess[:, pair], in_=bits, func=ACT.Identity, scale=-GUESS_SLOPE, bias=offset[:]
            )

        for k in range(4):
            nc.vector.tensor_scalar(
                out=neg_s[k][:], in0=z1[k][:], scalar1=neg_tp[:, k : k + 1], scalar2=None,
                op0=ALU.mult, op1=ALU.min, accum_out=neg_max[:, k : k + 1],
            )
            nc.scalar.activation(
                out=tanh_z2[k][:], in_=neg_s[k][:], func=ACT.Exp, scale=-1.0, bias=neg_max[:, k : k + 1],
                accum_out=total[:, k : k + 1],
            )
            if k >= 2:
                guess_log(pairs[k - 2])

        quantize(nc, w2_codes[:], w2_scales[:], w2_words[:])
        for h in range(2):
            for k in range(4):
                product(nc, banks[h][k][:, 0:HALF], w2_codes, w2_scales, x_codes, x_scales, k, h)
        for h in range(2):
            for k in range(4):
                nc.scalar.activation(
                    out=tanh_z2[k][:, halves[h]], in_=banks[h][k][:, 0:HALF], func=ACT.Tanh, scale=0.5
                )

        def make_gate(k, h):
            nc.vector.tensor_scalar(
                out=gate[k][:, halves[h]], in0=tanh_z2[k][:, halves[h]], scalar1=1.0,
                scalar2=neg_half_hs[:, k : k + 1], op0=ALU.add, op1=ALU.mult,
            )

        def add_times(result, a, number, b):
            nc.vector.scalar_tensor_tensor(out=result, in0=a, scalar=number, in1=b, op0=ALU.add, op1=ALU.mult)

        w, base, w_plus, w_minus = small("w"), small("base"), small("w_plus"), small("w_minus")
        below_part, above_part, below, above = small("below_part"), small("above_part"), small("below"), small("above")
        inverse, shift = small("inverse"), small("shift")

        def log_step(step, c):
            if step == 0:
                nc.vector.tensor_tensor(out=w[:, c], in0=total[:, c], in1=undo[:, c], op=ALU.mult)
                nc.vector.scalar_tensor_tensor(
                    out=base[:, c], in0=neg_guess[:, c], scalar=6.0, in1=neg_max[:, c], op0=ALU.add, op1=ALU.add
                )
            elif step == 1:
                add_times(below_part[:, c], w[:, c], 8.0, w[:, c])
                nc.vector.tensor_scalar(out=w_plus[:, c], in0=w[:, c], scalar1=1.0, scalar2=None, op0=ALU.add)
                add_times(above_part[:, c], w[:, c], 38.0 / 11.0, w[:, c])
                nc.vector.tensor_scalar(
                    out=w_minus[:, c], in0=w[:, c], scalar1=-1.0, scalar2=11.0 / 3.0, op0=ALU.add, op1=ALU.mult
                )
            elif step == 2:
                add_times(below[:, c], below_part[:, c], 1.0, w_plus[:, c])
                add_times(above[:, c], above_part[:, c], 1.0, w_minus[:, c])
            elif step == 3:
                nc.vector.reciprocal(out=inverse[:, c], in_=below[:, c])
            else:
                for k in range(c.start, c.stop):
                    nc.vector.tensor_scalar(
                        out=shift[:, k : k + 1], in0=inverse[:, k : k + 1], scalar1=above[:, k : k + 1],
                        scalar2=base[:, k : k + 1], op0=ALU.mult, op1=ALU.subtract,
                    )

        hh_rows = [sbuf("hh_rows%d" % h, [P, PACK, HALF], BF16) for h in range(2)]

        def make_hh(k, h):
            g, t = TILES[k]
            hh = sbuf("hh%d_%d" % (k, h), [P, HALF], BF16)
            nc.vector.scalar_tensor_tensor(
                out=hh[:], in0=neg_s[k][:, halves[h]], scalar=shift[:, k : k + 1], in1=gate[k][:, halves[h]],
                op0=ALU.add, op1=ALU.mult,
            )
            first = ROWS * g + QUAD * t
            nc.sync.dma_start(out=hh_rows[h][first : first + QUAD, :, :], in_=hh[:])

        early, late = pairs
        for step in range(3):
            log_step(step, early)
        log_step(0, late)
        log_step(3, early)
        log_step(1, late)
        make_gate(0, 0)
        log_step(4, early)
        log_step(2, late)
        make_gate(1, 0)
        log_step(3, late)
        make_hh(0, 0)
        log_step(4, late)
        make_gate(2, 0)
        make_hh(1, 0)
        make_gate(3, 0)
        make_hh(2, 0)
        make_gate(0, 1)
        make_hh(3, 0)
        for k in (1, 2, 3):
            nc.scalar.activation(
                out=gate[k][:, halves[1]], in_=tanh_z2[k][:, halves[1]], func=ACT.Identity,
                scale=neg_half_hs[:, k : k + 1], bias=neg_half_hs[:, k : k + 1],
            )
        for k in range(4):
            make_hh(k, 1)

        wo_words = sbuf("wo_words", [P, O, PACK], BF16)
        interleave(nc.scalar.copy, wo_words, wo_raw, 0, O)

        for h in range(2):
            hh_words = sbuf("hh_words%d" % h, [P, HALF, PACK], BF16)
            interleave(nc.vector.tensor_copy, hh_words, hh_rows[h], 0, CALL)
            if h == 0:
                interleave(nc.scalar.copy, hh_words, hh_rows[h], VECTOR_COLS, HALF)
                interleave(nc.vector.tensor_copy, hh_words, hh_rows[h], CALL, VECTOR_COLS)
                quantize(nc, wo_codes[:], wo_scales[:], wo_words[:])
            else:
                interleave(nc.vector.tensor_copy, hh_words, hh_rows[h], CALL, HALF)
            for first in range(0, HALF, CALL):
                cols = slice(HALF * h + first, HALF * h + first + CALL)
                quantize(nc, hh_codes[:, cols], hh_scales[:, cols], hh_words[:, first : first + CALL, :])
            for k in range(4):
                product(nc, banks[h][k][:, 0:HALF], wo_codes, wo_scales, hh_codes, hh_scales, k, h)

        for h in range(2):
            for k, (g, t) in enumerate(TILES):
                c = QUAD * (2 * g + t)
                squashed = sbuf("squashed%d_%d" % (k, h), [P, HALF], F32)
                nc.scalar.activation(
                    out=squashed[:], in_=banks[h][k][:, 0:HALF], func=ACT.Tanh, bias=vec[:, c + 2 : c + 3]
                )
                result = sbuf("result%d_%d" % (k, h), [P, HALF], F32)
                nc.vector.tensor_scalar(
                    out=result[:], in0=squashed[:], scalar1=vec[:, c + 3 : c + 4], scalar2=None, op0=ALU.mult
                )
                nc.sync.dma_start(out=out[g, P * t : P * (t + 1), halves[h]], in_=result[:])
